import numpy as np
import ml_dtypes


def mxq(x, axis, fmt="e4m3"):
    dtype, down = {"e4m3": (ml_dtypes.float8_e4m3fn, 7), "e5m2": (ml_dtypes.float8_e5m2, 14)}[fmt]
    v = np.moveaxis(np.asarray(x, np.float32).astype(ml_dtypes.bfloat16).astype(np.float64), axis, -1)
    blocks = v.reshape(v.shape[:-1] + (-1, 32))
    amax = np.abs(blocks).max(-1, keepdims=True)
    byte = np.maximum(np.where(amax > 0, np.frexp(amax)[1] - 1 + 127, 0) - down, 1)
    scale = np.exp2(byte - 127.0)
    codes = (blocks / scale).astype(np.float32).astype(dtype).astype(np.float64)
    return np.moveaxis((codes * scale).reshape(v.shape), -1, axis)


WIDE = False


def mx_kscale(k):
    if not WIDE:
        return np.ones(k)
    levels = np.array([10, -10, 5, -5, 0])
    if k % 512:
        return np.exp2(np.random.permutation(np.resize(levels, k // 32))).repeat(32)
    a = np.empty((k // 512, 16))
    for p in range(k // 512):
        a[p, :8] = np.random.permutation(np.resize(levels, 8))
        for g in range(8):
            far = levels[np.abs(levels - a[p, g]) >= 10]
            a[p, g + 8] = far[np.random.randint(len(far))]
    return np.exp2(a.ravel()).repeat(32)


def f64(x):
    return np.asarray(x).astype(np.float64)


def striped(idx):
    return np.tile(np.asarray(idx).reshape(-1, 16).T, (8, 1)).astype(np.uint16)


def unstriped(offs):
    return offs[:16].T.reshape(-1).astype(np.int64)


def striped8(idx):
    return np.asarray(idx).reshape(8, -1, 16).transpose(0, 2, 1).reshape(128, -1).astype(np.uint16)


def unstriped8(offs):
    return offs.reshape(8, 16, -1).transpose(0, 2, 1).reshape(8, -1).astype(np.int64)


def pick8(x, idx, run):
    r = np.arange(len(x))
    return x[r[:, None], idx[r % (8 * run) // run]]


E2M1 = np.array([0.0, 0.5, 1.0, 1.5, 2.0, 3.0, 4.0, 6.0, -0.0, -0.5, -1.0, -1.5, -2.0, -3.0, -4.0, -6.0])


def pack_weight(w, fmt):
    k, n = w.shape
    w = f64(np.asarray(w, np.float32).astype(ml_dtypes.bfloat16)).reshape(k // 32, 32, n)
    amax = np.abs(w).max(1)
    if fmt == "e4m3":
        byte = np.frexp(amax)[1] - 1 + 127 - 7
    else:
        mant, ex = np.frexp(amax / 6.0)
        byte = np.where(mant > 0.5, ex, ex - 1) + 127
    byte = np.clip(np.where(amax > 0, byte, 1), 1, 254)
    scaled = (w * np.exp2(127.0 - byte)[:, None, :]).reshape(k, n).astype(np.float32)
    by_word = np.ascontiguousarray(scaled.reshape(k // 512, 128, 4, n).transpose(0, 1, 3, 2))
    if fmt == "e4m3":
        words = by_word.astype(ml_dtypes.float8_e4m3fn).view(np.uint8)
    else:
        c = by_word.astype(ml_dtypes.float4_e2m1fn).view(np.uint8) & 0xF
        words = (c[..., 0::2] | (c[..., 1::2] << 4)).reshape(k // 512, 128, 2 * n)
    return np.ascontiguousarray(words), np.ascontiguousarray(byte.astype(np.uint8).reshape(k // 512, 16, n))


def unpack_weight(words, scales, fmt):
    g, _, n = scales.shape
    words = np.ascontiguousarray(words).reshape(g, 128, n, -1)
    if fmt == "e4m3":
        vals = words.view(ml_dtypes.float8_e4m3fn).astype(np.float64)
    else:
        nib = np.empty((g, 128, n, 4), np.uint8)
        nib[..., 0::2] = words & 0xF
        nib[..., 1::2] = words >> 4
        vals = E2M1[nib]
    vals = vals * np.repeat(np.exp2(scales.astype(np.float64) - 127.0), 8, axis=1)[..., None]
    return vals.transpose(0, 1, 3, 2).reshape(g * 512, n)


K, J, R, T, U, F, C, O, N, S = 512, 256, 512, 1024, 512, 1024, 512, 128, 256, 1024


def setup_inputs():
    n = np.random.standard_normal
    idx = np.stack([np.random.permutation(T)[:U] for _ in range(8)])
    idx2 = np.random.permutation(U)[:J]
    idx3 = np.random.permutation(F)[:R]
    idx4 = np.random.permutation(C)[:J]
    idx5 = np.random.permutation(C)[:O]
    idx6 = np.stack([np.random.permutation(C)[:O] for _ in range(8)])
    idx7 = np.random.permutation(S)[:N]
    fk = mx_kscale(K)
    fr = mx_kscale(R)
    tr = np.ones(F)
    tr[idx3] = fr
    wtp = pack_weight(n((K, F)) * 1 / np.sqrt(K) / fk[:, None] * tr, "e4m3")
    vsp = pack_weight(n((R, S)) * 1 / np.sqrt(R) / fr[:, None], "e2m1")
    return {
        "ta": (np.random.randint(-7, 8, (K, T)).astype(np.float64)).astype(np.float32),
        "ga": ((np.random.randint(8, 25, (K, 1)) / 64.0) * fk[:, None]).astype(np.float32),
        "gb": (np.random.uniform(0.5, 1.6, (K, 1))).astype(np.float32),
        "wt_words": wtp[0],
        "wt_scales": wtp[1],
        "sa": (np.random.uniform(0.5, 1.6, (R, 1))).astype(np.float32),
        "sb": (np.random.uniform(0.5, 1.6, (R, 1))).astype(np.float32),
        "vs_words": vsp[0],
        "vs_scales": vsp[1],
        "offs": striped8(idx),
        "offs2": striped(idx2),
        "offs3": striped(idx3),
        "offs4": striped(idx4),
        "offs5": striped(idx5),
        "offs6": striped8(idx6),
        "offs7": striped(idx7),
    }


def reference(ta, ga, gb, wt_words, wt_scales, sa, sb, vs_words, vs_scales, offs, offs2, offs3, offs4, offs5, offs6, offs7):
    idx = unstriped8(offs)
    idx2 = unstriped(offs2)
    idx3 = unstriped(offs3)
    idx4 = unstriped(offs4)
    idx5 = unstriped(offs5)
    idx6 = unstriped8(offs6)
    idx7 = unstriped(offs7)
    wtu = unpack_weight(wt_words, wt_scales, "e4m3")
    vsu = unpack_weight(vs_words, vs_scales, "e2m1")
    xcd = pick8(f64(ta), idx, 64) * f64(ga)
    xc = xcd[:, idx2] * f64(gb)
    wtidx3g = wtu[:, idx3]
    xcq = mxq(xc, 0, "e4m3")
    a = wtidx3g.T @ xcq
    pw = np.zeros((R, C))
    pw[:, idx4] = a
    hid = np.abs(pw[:, idx5] * f64(sa) - pick8(pw, idx6, 64) * f64(sb))
    vsidx7g = vsu[:, idx7]
    hidq = mxq(hid, 0, "e4m3")
    y = vsidx7g.T @ hidq
    return y

@@ -1,0 +1,199 @@
+from contextlib import ExitStack
+
+import concourse.mybir as mybir
+
+K, J, R, T, U, F, C, O, N, S = 512, 256, 512, 1024, 512, 1024, 512, 128, 256, 1024
+FLOPS = 2 * K * R * J + 2 * R * N * O
+
+F32 = mybir.dt.float32
+BF16 = mybir.dt.bfloat16
+I32 = mybir.dt.int32
+U32 = mybir.dt.uint32
+U16 = mybir.dt.uint16
+U8 = mybir.dt.uint8
+FP8X4 = mybir.dt.float8_e4m3fn_x4
+FP4X4 = mybir.dt.float4_e2m1fn_x4
+COPY = mybir.ActivationFunctionType.Copy
+ABS = mybir.ActivationFunctionType.Abs
+SUB = mybir.AluOpType.subtract
+
+P = 128
+PACK = 4
+HALF = J // 2
+PER_COL = 16
+
+
+def tile_picked_respelled_store_one_boardmixed_store_plain_kernel(
+    tc, ta, ga, gb, wt_words, wt_scales, sa, sb, vs_words, vs_scales, offs, offs2, offs3, offs4, offs5, offs6, offs7, out
+):
+    nc = tc.nc
+    with ExitStack() as ctx:
+        lists = ctx.enter_context(tc.tile_pool(name="lists", bufs=1))
+        keep = ctx.enter_context(tc.tile_pool(name="keep", bufs=1))
+        psum = ctx.enter_context(tc.psum_pool(name="psum", bufs=1))
+
+        def load_list(src, name):
+            tl = lists.tile([P, src.shape[1]], U16, name=name)
+            nc.sync.dma_start(tl[:], src)
+            return tl
+
+        def load_rowvals(src, name, queue):
+            tl = keep.tile([P, PACK], F32, name=name, tag=name)
+            queue.dma_start(tl[:], src.rearrange("(p t) o -> p (t o)", t=PACK))
+            return tl
+
+        ta_rows = ta.rearrange("(p t) c -> p t c", t=PACK)
+
+        def load_ta(t):
+            tl = keep.tile([P, T], F32, name="ta%d" % t, tag="ta%d" % t)
+            nc.sync.dma_start(tl[:], ta_rows[:, t, :])
+            return tl
+
+        def load_scale_rows(src, name):
+            tl = keep.tile([4, 4, 256], I32, name=name)
+            nc.gpsimd.dma_start(tl[:], src[0].rearrange("(q j) c -> j q c", j=4).bitcast(I32))
+            return tl
+
+        l1 = load_list(offs, "l1")
+        ga_t = load_rowvals(ga, "ga_t", nc.scalar)
+        ta_t = [load_ta(0)]
+        l2 = load_list(offs2, "l2")
+        gb_t = [load_rowvals(gb, "gb0", nc.scalar)]
+        wt_stage = load_scale_rows(wt_scales, "wt_stage")
+        vs_stage = load_scale_rows(vs_scales, "vs_stage")
+        gb_t.append(load_rowvals(gb, "gb1", nc.gpsimd))
+        sa_t = load_rowvals(sa, "sa_t", nc.gpsimd)
+        sb_t = load_rowvals(sb, "sb_t", nc.gpsimd)
+        ta_t.append(load_ta(1))
+        l3 = load_list(offs3, "l3")
+        ta_t.append(load_ta(2))
+        l7 = load_list(offs7, "l7")
+        ta_t.append(load_ta(3))
+        wt_win = keep.tile([P, F], I32, name="wt_win", tag="wt_win", align_bytes=64)
+        nc.sync.dma_start(wt_win[:], wt_words[0].rearrange("p n t -> p (n t)").bitcast(I32))
+        vs_win = keep.tile([P, S // 2], I32, name="vs_win")
+        nc.sync.dma_start(vs_win[:], vs_words[0].bitcast(I32))
+        l4 = load_list(offs4, "l4")
+        l5 = load_list(offs5, "l5")
+        l6 = load_list(offs6, "l6")
+
+        wt_swin = keep.tile([P, 256], I32, name="wt_swin")
+        vs_swin = keep.tile([P, 256], I32, name="vs_swin")
+        nc.vector.memset(wt_swin[:], 0)
+        nc.vector.memset(vs_swin[:], 0)
+        pw = []
+        for t in range(PACK):
+            tl = keep.tile([P, C], F32, name="pw%d" % t)
+            nc.vector.memset(tl[:], 0.0)
+            pw.append(tl)
+
+        def spread(win, stage):
+            for q in range(4):
+                nc.vector.tensor_copy(win[32 * q : 32 * q + 4, :], stage[:, q, :])
+
+        spread(wt_swin, wt_stage)
+        wt_s = keep.tile([P, PACK, P], U8, name="wt_s", align_bytes=64)
+        nc.vector.tensor_copy(wt_s[:].rearrange("p t m -> p m t"), wt_swin[:].bitcast(U8).indirect(l3[:]))
+        wt_w = keep.tile([P, PACK, P], U32, name="wt_w", align_bytes=64)
+        nc.vector.tensor_copy(wt_w[:].rearrange("p t m -> p m t"), wt_win[:].bitcast(U32).indirect(l3[:]))
+        spread(vs_swin, vs_stage)
+        vs_s = keep.tile([P, N], U8, name="vs_s", align_bytes=64)
+        nc.vector.tensor_copy(vs_s[:], vs_swin[:].bitcast(U8).indirect(l7[:]))
+
+        hc = HALF // PER_COL
+        xc = []
+        xcd = []
+
+        def read_slots(t, h):
+            nc.scalar.activation(xc[h][:, t, :], xcd[t][:].indirect(l2[:, h * hc : (h + 1) * hc]), COPY, scale=gb_t[h][:, t : t + 1])
+
+        for t in range(PACK):
+            tl = keep.tile([P, U], F32, name="xcd%d" % t)
+            nc.scalar.activation(tl[:], ta_t[t][:].indirect(l1[:]), COPY, scale=ga_t[:, t : t + 1])
+            xcd.append(tl)
+        xc.append(keep.tile([P, PACK, HALF], BF16, name="xc0", tag="ta3"))
+        for t in range(PACK):
+            read_slots(t, 0)
+
+        def first_product(h):
+            woven = keep.tile([P, HALF, PACK], BF16, name="xw%d" % h, tag="wt_win", align_bytes=64)
+            for t0, t1 in ((0, 2), (2, 4)) if h == 0 else ((0, 4),):
+                nc.vector.tensor_copy(
+                    woven[:, :, t0:t1].rearrange("p (c i) t -> p c t i", i=4),
+                    xc[h][:, t0:t1, :].rearrange("p t (c i) -> p c t i", i=4),
+                )
+            codes = keep.tile([P, HALF], U32, name="xq%d" % h, align_bytes=64)
+            scales = keep.tile([P, HALF], U8, name="xs%d" % h, align_bytes=64)
+            nc.vector.quantize_mx(out=codes[:].bitcast(FP8X4), scales=scales[:], in_=woven[:].rearrange("p c t -> p (c t)"))
+            acc = [psum.tile([P, 2, HALF], F32, name="acc%d_%d" % (h, u)) for u in range(2)]
+            for t in range(PACK):
+                nc.tensor.matmul_mx(
+                    out=acc[t // 2][:, t % 2, :], lhsT=wt_w[:, t, :].bitcast(FP8X4), lhsT_scale=wt_s[:, t, :],
+                    rhs=codes[:].bitcast(FP8X4), rhs_scale=scales[:], start=True, stop=True,
+                )
+            return acc
+
+        acc0 = first_product(0)
+        xc.append(keep.tile([P, PACK, HALF], BF16, name="xc1", tag="gb0"))
+        for t in range(PACK):
+            read_slots(t, 1)
+        acc1 = first_product(1)
+
+        a = [[keep.tile([P, 2, HALF], F32, name="a%d_%d" % (h, u), tag="a%d_%d" % (h, u), align_bytes=64) for u in range(2)] for h in range(2)]
+
+        def put(t, h, on_scalar):
+            dst = pw[t][:].indirect(l4[:, h * hc : (h + 1) * hc])
+            if on_scalar:
+                nc.scalar.activation(dst, a[h][t // 2][:, t % 2, :], COPY)
+            else:
+                nc.vector.tensor_copy(dst, a[h][t // 2][:, t % 2, :])
+
+        first = keep.tile([P, PACK, O], F32, name="first")
+        second = keep.tile([P, PACK, O], F32, name="second")
+        diff = keep.tile([P, PACK, O], F32, name="diff")
+
+        def read_board(t):
+            nc.scalar.activation(first[:, t, :], pw[t][:].indirect(l5[:]), COPY, scale=sa_t[:, t : t + 1])
+            nc.scalar.activation(second[:, t, :], pw[t][:].indirect(l6[:]), COPY, scale=sb_t[:, t : t + 1])
+
+        nc.scalar.copy(a[0][0][:], acc0[0][:])
+        nc.vector.tensor_copy(a[0][1][:], acc0[1][:])
+        put(0, 0, True)
+        put(1, 0, False)
+        put(3, 0, True)
+        nc.vector.tensor_copy(a[1][0][:], acc1[0][:])
+        put(2, 0, False)
+        nc.vector.tensor_copy(a[1][1][:], acc1[1][:])
+        put(0, 1, True)
+        put(1, 1, False)
+        read_board(0)
+        put(2, 1, False)
+        read_board(1)
+        put(3, 1, False)
+        vs_w = keep.tile([P, 2 * N], U8, name="vs_w", tag="a1_1", align_bytes=64)
+        nc.vector.tensor_copy(vs_w[:].bitcast(U16), vs_win[:].bitcast(U16).indirect(l7[:]))
+        read_board(2)
+        nc.vector.tensor_tensor(diff[:, 0:3, :], first[:, 0:3, :], second[:, 0:3, :], SUB)
+        read_board(3)
+        nc.vector.tensor_tensor(diff[:, 3, :], first[:, 3, :], second[:, 3, :], SUB)
+
+        hid = keep.tile([P, O, PACK], BF16, name="hid", align_bytes=64)
+        nc.scalar.activation(
+            hid[:].rearrange("p (c i) t -> p c t i", i=4), diff[:].rearrange("p t (c i) -> p c t i", i=4), ABS
+        )
+        hq = keep.tile([P, O], U32, name="hq", align_bytes=64)
+        hs = keep.tile([P, O], U8, name="hs", align_bytes=64)
+        nc.vector.quantize_mx(out=hq[:].bitcast(FP8X4), scales=hs[:], in_=hid[:].rearrange("p c t -> p (c t)"))
+        for i in range(2):
+            y = psum.tile([P, O], F32, name="y%d" % i)
+            nc.tensor.matmul_mx(
+                out=y[:], lhsT=vs_w[:, 2 * P * i : 2 * P * (i + 1)].bitcast(FP4X4), lhsT_scale=vs_s[:, P * i : P * (i + 1)],
+                rhs=hq[:].bitcast(FP8X4), rhs_scale=hs[:], start=True, stop=True,
+            )
+            res = keep.tile([P, O], F32, name="res%d" % i)
+            if i == 0:
+                nc.vector.tensor_copy(res[:], y[:])
+                nc.sync.dma_start(out[P * i : P * (i + 1), :], res[:])
+            else:
+                nc.scalar.copy(res[:], y[:])
+                nc.scalar.dma_start(out[P * i : P * (i + 1), :], res[:])

@@ -102,6 +102,9 @@ def tile_picked_respelled_store_one_boardmixed_store_plain_kernel(
 
         hc = HALF // PER_COL
         xc = []
+        warm = keep.tile([P, 2], F32, name="warm")
+        nc.vector.memset(warm[:, 0:1], 0.0)
+        nc.scalar.activation(warm[:, 1:2], warm[:, 0:1], COPY)
         xcd = []
 
         def read_slots(t, h):

@@ -16,6 +16,8 @@ FP4X4 = mybir.dt.float4_e2m1fn_x4
 COPY = mybir.ActivationFunctionType.Copy
 ABS = mybir.ActivationFunctionType.Abs
 SUB = mybir.AluOpType.subtract
+MULT = mybir.AluOpType.mult
+MAX = mybir.AluOpType.max
 
 P = 128
 PACK = 4
@@ -49,62 +51,54 @@ def tile_picked_respelled_store_one_boardmixed_store_plain_kernel(
             nc.sync.dma_start(tl[:], ta_rows[:, t, :])
             return tl
 
-        def load_scale_rows(src, name):
-            tl = keep.tile([4, 4, 256], I32, name=name)
-            nc.gpsimd.dma_start(tl[:], src[0].rearrange("(q j) c -> j q c", j=4).bitcast(I32))
+        def load_scale_rows(src, name, clear):
+            tl = keep.tile([P, 256], I32, name=name, tag=name, align_bytes=64)
+            clear.memset(tl[:], 0)
+            rows = src[0].rearrange("(q j) c -> j q c", j=4).bitcast(I32)
+            for j in range(4):
+                nc.sync.dma_start(tl[j:P:32, :], rows[j])
             return tl
 
         l1 = load_list(offs, "l1")
         ga_t = load_rowvals(ga, "ga_t", nc.scalar)
-        ta_t = [load_ta(0)]
-        l2 = load_list(offs2, "l2")
-        gb_t = [load_rowvals(gb, "gb0", nc.scalar)]
-        wt_stage = load_scale_rows(wt_scales, "wt_stage")
-        vs_stage = load_scale_rows(vs_scales, "vs_stage")
-        gb_t.append(load_rowvals(gb, "gb1", nc.gpsimd))
-        sa_t = load_rowvals(sa, "sa_t", nc.gpsimd)
-        sb_t = load_rowvals(sb, "sb_t", nc.gpsimd)
-        ta_t.append(load_ta(1))
+        ta_t = [load_ta(0), load_ta(1)]
+        wt_swin = load_scale_rows(wt_scales, "wt_swin", nc.gpsimd)
         l3 = load_list(offs3, "l3")
         ta_t.append(load_ta(2))
-        l7 = load_list(offs7, "l7")
-        ta_t.append(load_ta(3))
-        wt_win = keep.tile([P, F], I32, name="wt_win", tag="wt_win", align_bytes=64)
+        wt_win = keep.tile([P, F], I32, name="wt_win")
         nc.sync.dma_start(wt_win[:], wt_words[0].rearrange("p n t -> p (n t)").bitcast(I32))
+        l2 = load_list(offs2, "l2")
+        gb_t = [load_rowvals(gb, "gb0", nc.sync)]
+        ta_t.append(load_ta(3))
+        l7 = load_list(offs7, "l7")
         vs_win = keep.tile([P, S // 2], I32, name="vs_win")
         nc.sync.dma_start(vs_win[:], vs_words[0].bitcast(I32))
+        vs_swin = load_scale_rows(vs_scales, "vs_swin", nc.vector)
         l4 = load_list(offs4, "l4")
         l5 = load_list(offs5, "l5")
         l6 = load_list(offs6, "l6")
+        sa_t = load_rowvals(sa, "sa_t", nc.sync)
+        sb_t = load_rowvals(sb, "sb_t", nc.sync)
+        gb_t.append(keep.tile([P, PACK], F32, name="gb1"))
+        nc.vector.tensor_copy(gb_t[1][:], gb_t[0][:])
 
-        wt_swin = keep.tile([P, 256], I32, name="wt_swin")
-        vs_swin = keep.tile([P, 256], I32, name="vs_swin")
-        nc.vector.memset(wt_swin[:], 0)
-        nc.vector.memset(vs_swin[:], 0)
         pw = []
         for t in range(PACK):
             tl = keep.tile([P, C], F32, name="pw%d" % t)
             nc.vector.memset(tl[:], 0.0)
             pw.append(tl)
 
-        def spread(win, stage):
-            for q in range(4):
-                nc.vector.tensor_copy(win[32 * q : 32 * q + 4, :], stage[:, q, :])
-
-        spread(wt_swin, wt_stage)
         wt_s = keep.tile([P, PACK, P], U8, name="wt_s", align_bytes=64)
         nc.vector.tensor_copy(wt_s[:].rearrange("p t m -> p m t"), wt_swin[:].bitcast(U8).indirect(l3[:]))
         wt_w = keep.tile([P, PACK, P], U32, name="wt_w", align_bytes=64)
         nc.vector.tensor_copy(wt_w[:].rearrange("p t m -> p m t"), wt_win[:].bitcast(U32).indirect(l3[:]))
-        spread(vs_swin, vs_stage)
+        vs_w = keep.tile([P, 2 * N], U8, name="vs_w", align_bytes=64)
+        nc.vector.tensor_copy(vs_w[:].bitcast(U16), vs_win[:].bitcast(U16).indirect(l7[:]))
         vs_s = keep.tile([P, N], U8, name="vs_s", align_bytes=64)
         nc.vector.tensor_copy(vs_s[:], vs_swin[:].bitcast(U8).indirect(l7[:]))
 
         hc = HALF // PER_COL
         xc = []
-        warm = keep.tile([P, 2], F32, name="warm")
-        nc.vector.memset(warm[:, 0:1], 0.0)
-        nc.scalar.activation(warm[:, 1:2], warm[:, 0:1], COPY)
         xcd = []
 
         def read_slots(t, h):
@@ -114,13 +108,17 @@ def tile_picked_respelled_store_one_boardmixed_store_plain_kernel(
             tl = keep.tile([P, U], F32, name="xcd%d" % t)
             nc.scalar.activation(tl[:], ta_t[t][:].indirect(l1[:]), COPY, scale=ga_t[:, t : t + 1])
             xcd.append(tl)
-        xc.append(keep.tile([P, PACK, HALF], BF16, name="xc0", tag="ta3"))
+        xc.append(keep.tile([P, PACK, HALF], BF16, name="xc0", tag="ta2"))
         for t in range(PACK):
             read_slots(t, 0)
 
+        place = {(0, 0): (0, 0), (1, 0): (0, 1), (0, 1): (1, 0), (1, 1): (1, 1),
+                 (2, 0): (2, 0), (2, 1): (2, 1), (3, 0): (3, 0), (3, 1): (3, 1)}
+        acc = [psum.tile([P, 2, HALF], F32, name="acc%d" % b) for b in range(4)]
+
         def first_product(h):
-            woven = keep.tile([P, HALF, PACK], BF16, name="xw%d" % h, tag="wt_win", align_bytes=64)
-            for t0, t1 in ((0, 2), (2, 4)) if h == 0 else ((0, 4),):
+            woven = keep.tile([P, HALF, PACK], BF16, name="xw%d" % h, tag="vs_swin", align_bytes=64)
+            for t0, t1 in ((0, 2), (2, 4)):
                 nc.vector.tensor_copy(
                     woven[:, :, t0:t1].rearrange("p (c i) t -> p c t i", i=4),
                     xc[h][:, t0:t1, :].rearrange("p t (c i) -> p c t i", i=4),
@@ -128,28 +126,27 @@ def tile_picked_respelled_store_one_boardmixed_store_plain_kernel(
             codes = keep.tile([P, HALF], U32, name="xq%d" % h, align_bytes=64)
             scales = keep.tile([P, HALF], U8, name="xs%d" % h, align_bytes=64)
             nc.vector.quantize_mx(out=codes[:].bitcast(FP8X4), scales=scales[:], in_=woven[:].rearrange("p c t -> p (c t)"))
-            acc = [psum.tile([P, 2, HALF], F32, name="acc%d_%d" % (h, u)) for u in range(2)]
             for t in range(PACK):
                 nc.tensor.matmul_mx(
-                    out=acc[t // 2][:, t % 2, :], lhsT=wt_w[:, t, :].bitcast(FP8X4), lhsT_scale=wt_s[:, t, :],
+                    out=acc[place[t, h][0]][:, place[t, h][1], :], lhsT=wt_w[:, t, :].bitcast(FP8X4), lhsT_scale=wt_s[:, t, :],
                     rhs=codes[:].bitcast(FP8X4), rhs_scale=scales[:], start=True, stop=True,
                 )
-            return acc
 
-        acc0 = first_product(0)
+        first_product(0)
         xc.append(keep.tile([P, PACK, HALF], BF16, name="xc1", tag="gb0"))
         for t in range(PACK):
             read_slots(t, 1)
-        acc1 = first_product(1)
+        first_product(1)
 
-        a = [[keep.tile([P, 2, HALF], F32, name="a%d_%d" % (h, u), tag="a%d_%d" % (h, u), align_bytes=64) for u in range(2)] for h in range(2)]
+        a = [keep.tile([P, 2, HALF], F32, name="a%d" % b) for b in range(4)]
 
         def put(t, h, on_scalar):
             dst = pw[t][:].indirect(l4[:, h * hc : (h + 1) * hc])
+            src = a[place[t, h][0]][:, place[t, h][1], :]
             if on_scalar:
-                nc.scalar.activation(dst, a[h][t // 2][:, t % 2, :], COPY)
+                nc.scalar.activation(dst, src, COPY)
             else:
-                nc.vector.tensor_copy(dst, a[h][t // 2][:, t % 2, :])
+                nc.vector.tensor_copy(dst, src)
 
         first = keep.tile([P, PACK, O], F32, name="first")
         second = keep.tile([P, PACK, O], F32, name="second")
@@ -159,31 +156,30 @@ def tile_picked_respelled_store_one_boardmixed_store_plain_kernel(
             nc.scalar.activation(first[:, t, :], pw[t][:].indirect(l5[:]), COPY, scale=sa_t[:, t : t + 1])
             nc.scalar.activation(second[:, t, :], pw[t][:].indirect(l6[:]), COPY, scale=sb_t[:, t : t + 1])
 
-        nc.scalar.copy(a[0][0][:], acc0[0][:])
-        nc.vector.tensor_copy(a[0][1][:], acc0[1][:])
+        hid = keep.tile([P, O, PACK], BF16, name="hid", align_bytes=64)
+        for u in range(2):
+            nc.scalar.copy(a[0][:, u, :], acc[0][:, u, :])
         put(0, 0, True)
         put(1, 0, False)
-        put(3, 0, True)
-        nc.vector.tensor_copy(a[1][0][:], acc1[0][:])
-        put(2, 0, False)
-        nc.vector.tensor_copy(a[1][1][:], acc1[1][:])
+        for u in range(2):
+            nc.scalar.copy(a[1][:, u, :], acc[1][:, u, :])
+        nc.vector.tensor_copy(a[2][:], acc[2][:])
+        nc.vector.tensor_copy(a[3][:], acc[3][:])
         put(0, 1, True)
         put(1, 1, False)
+        put(3, 0, True)
+        nc.vector.tensor_copy(pw[2][:].indirect(l4[:]), a[2][:].rearrange("p h j -> p (h j)"))
         read_board(0)
-        put(2, 1, False)
-        read_board(1)
         put(3, 1, False)
-        vs_w = keep.tile([P, 2 * N], U8, name="vs_w", tag="a1_1", align_bytes=64)
-        nc.vector.tensor_copy(vs_w[:].bitcast(U16), vs_win[:].bitcast(U16).indirect(l7[:]))
+        read_board(1)
+        nc.vector.tensor_tensor(diff[:, 0:2, :], first[:, 0:2, :], second[:, 0:2, :], SUB)
         read_board(2)
-        nc.vector.tensor_tensor(diff[:, 0:3, :], first[:, 0:3, :], second[:, 0:3, :], SUB)
+        nc.vector.tensor_tensor(diff[:, 2, :], first[:, 2, :], second[:, 2, :], SUB)
+        low = diff[:, 0:2, :].rearrange("p t o -> p o t")
+        nc.vector.scalar_tensor_tensor(hid[:, :, 0:2], low, -1.0, low, MULT, MAX)
         read_board(3)
         nc.vector.tensor_tensor(diff[:, 3, :], first[:, 3, :], second[:, 3, :], SUB)
-
-        hid = keep.tile([P, O, PACK], BF16, name="hid", align_bytes=64)
-        nc.scalar.activation(
-            hid[:].rearrange("p (c i) t -> p c t i", i=4), diff[:].rearrange("p t (c i) -> p c t i", i=4), ABS
-        )
+        nc.scalar.activation(hid[:, :, 2:4], diff[:, 2:4, :].rearrange("p t o -> p o t"), ABS)
         hq = keep.tile([P, O], U32, name="hq", align_bytes=64)
         hs = keep.tile([P, O], U8, name="hs", align_bytes=64)
         nc.vector.quantize_mx(out=hq[:].bitcast(FP8X4), scales=hs[:], in_=hid[:].rearrange("p c t -> p (c t)"))

@@ -99,6 +99,9 @@ def tile_picked_respelled_store_one_boardmixed_store_plain_kernel(
 
         hc = HALF // PER_COL
         xc = []
+        warm = keep.tile([P, 2], F32, name="warm")
+        nc.gpsimd.memset(warm[:, 0:1], 0.0)
+        nc.scalar.activation(warm[:, 1:2], warm[:, 0:1], COPY)
         xcd = []
 
         def read_slots(t, h):

@@ -20,9 +20,11 @@ MULT = mybir.AluOpType.mult
 MAX = mybir.AluOpType.max
 
 P = 128
-PACK = 4
+PLANES = 4
+QUADRANT = 32
 HALF = J // 2
-PER_COL = 16
+HALF_COLS = HALF // 16
+MX_ALIGN = 64
 
 
 def tile_picked_respelled_store_one_boardmixed_store_plain_kernel(
@@ -39,163 +41,170 @@ def tile_picked_respelled_store_one_boardmixed_store_plain_kernel(
             nc.sync.dma_start(tl[:], src)
             return tl
 
-        def load_rowvals(src, name, queue):
-            tl = keep.tile([P, PACK], F32, name=name, tag=name)
-            queue.dma_start(tl[:], src.rearrange("(p t) o -> p (t o)", t=PACK))
+        def load_row_values(src, name, queue):
+            tl = keep.tile([P, PLANES], F32, name=name, tag=name)
+            queue.dma_start(tl[:], src.rearrange("(p t) o -> p (t o)", t=PLANES))
             return tl
 
-        ta_rows = ta.rearrange("(p t) c -> p t c", t=PACK)
+        ta_rows = ta.rearrange("(p t) c -> p t c", t=PLANES)
 
-        def load_ta(t):
+        def load_table_plane(t):
             tl = keep.tile([P, T], F32, name="ta%d" % t, tag="ta%d" % t)
             nc.sync.dma_start(tl[:], ta_rows[:, t, :])
             return tl
 
-        def load_scale_rows(src, name, clear):
-            tl = keep.tile([P, 256], I32, name=name, tag=name, align_bytes=64)
-            clear.memset(tl[:], 0)
+        def load_scale_rows(src, name, clearing_engine):
+            tl = keep.tile([P, src.shape[2] // 4], I32, name=name, tag=name, align_bytes=MX_ALIGN)
+            clearing_engine.memset(tl[:], 0)
             rows = src[0].rearrange("(q j) c -> j q c", j=4).bitcast(I32)
             for j in range(4):
-                nc.sync.dma_start(tl[j:P:32, :], rows[j])
+                nc.sync.dma_start(tl[j:P:QUADRANT, :], rows[j])
             return tl
 
-        l1 = load_list(offs, "l1")
-        ga_t = load_rowvals(ga, "ga_t", nc.scalar)
-        ta_t = [load_ta(0), load_ta(1)]
-        wt_swin = load_scale_rows(wt_scales, "wt_swin", nc.gpsimd)
-        l3 = load_list(offs3, "l3")
-        ta_t.append(load_ta(2))
-        wt_win = keep.tile([P, F], I32, name="wt_win")
-        nc.sync.dma_start(wt_win[:], wt_words[0].rearrange("p n t -> p (n t)").bitcast(I32))
-        l2 = load_list(offs2, "l2")
-        gb_t = [load_rowvals(gb, "gb0", nc.sync)]
-        ta_t.append(load_ta(3))
-        l7 = load_list(offs7, "l7")
-        vs_win = keep.tile([P, S // 2], I32, name="vs_win")
-        nc.sync.dma_start(vs_win[:], vs_words[0].bitcast(I32))
-        vs_swin = load_scale_rows(vs_scales, "vs_swin", nc.vector)
-        l4 = load_list(offs4, "l4")
-        l5 = load_list(offs5, "l5")
-        l6 = load_list(offs6, "l6")
-        sa_t = load_rowvals(sa, "sa_t", nc.sync)
-        sb_t = load_rowvals(sb, "sb_t", nc.sync)
-        gb_t.append(keep.tile([P, PACK], F32, name="gb1"))
-        nc.vector.tensor_copy(gb_t[1][:], gb_t[0][:])
-
-        pw = []
-        for t in range(PACK):
-            tl = keep.tile([P, C], F32, name="pw%d" % t)
-            nc.vector.memset(tl[:], 0.0)
-            pw.append(tl)
-
-        wt_s = keep.tile([P, PACK, P], U8, name="wt_s", align_bytes=64)
-        nc.vector.tensor_copy(wt_s[:].rearrange("p t m -> p m t"), wt_swin[:].bitcast(U8).indirect(l3[:]))
-        wt_w = keep.tile([P, PACK, P], U32, name="wt_w", align_bytes=64)
-        nc.vector.tensor_copy(wt_w[:].rearrange("p t m -> p m t"), wt_win[:].bitcast(U32).indirect(l3[:]))
-        vs_w = keep.tile([P, 2 * N], U8, name="vs_w", align_bytes=64)
-        nc.vector.tensor_copy(vs_w[:].bitcast(U16), vs_win[:].bitcast(U16).indirect(l7[:]))
-        vs_s = keep.tile([P, N], U8, name="vs_s", align_bytes=64)
-        nc.vector.tensor_copy(vs_s[:], vs_swin[:].bitcast(U8).indirect(l7[:]))
-
-        hc = HALF // PER_COL
-        xc = []
         warm = keep.tile([P, 2], F32, name="warm")
         nc.gpsimd.memset(warm[:, 0:1], 0.0)
         nc.scalar.activation(warm[:, 1:2], warm[:, 0:1], COPY)
+
+        spell_list = load_list(offs, "spell_list")
+        ga_t = load_row_values(ga, "ga_t", nc.scalar)
+        table = [load_table_plane(0), load_table_plane(1)]
+        wt_scale_win = load_scale_rows(wt_scales, "wt_scale_win", nc.gpsimd)
+        wt_list = load_list(offs3, "wt_list")
+        table.append(load_table_plane(2))
+        wt_word_win = keep.tile([P, F], I32, name="wt_word_win")
+        nc.sync.dma_start(wt_word_win[:], wt_words[0].rearrange("p n t -> p (n t)").bitcast(I32))
+        slot_list = load_list(offs2, "slot_list")
+        gb_t = [load_row_values(gb, "gb0", nc.sync)]
+        table.append(load_table_plane(3))
+        vs_list = load_list(offs7, "vs_list")
+        vs_word_win = keep.tile([P, S // 2], I32, name="vs_word_win")
+        nc.sync.dma_start(vs_word_win[:], vs_words[0].bitcast(I32))
+        vs_scale_win = load_scale_rows(vs_scales, "vs_scale_win", nc.vector)
+        put_list = load_list(offs4, "put_list")
+        first_list = load_list(offs5, "first_list")
+        second_list = load_list(offs6, "second_list")
+        sa_t = load_row_values(sa, "sa_t", nc.sync)
+        sb_t = load_row_values(sb, "sb_t", nc.sync)
+        gb_t.append(keep.tile([P, PLANES], F32, name="gb1"))
+        nc.vector.tensor_copy(gb_t[1][:], gb_t[0][:])
+
+        board = []
+        for t in range(PLANES):
+            tl = keep.tile([P, C], F32, name="board%d" % t)
+            nc.vector.memset(tl[:], 0.0)
+            board.append(tl)
+
+        wt_s = keep.tile([P, PLANES, P], U8, name="wt_s", align_bytes=MX_ALIGN)
+        nc.vector.tensor_copy(wt_s[:].rearrange("p t m -> p m t"), wt_scale_win[:].bitcast(U8).indirect(wt_list[:]))
+        wt_w = keep.tile([P, PLANES, P], U32, name="wt_w", align_bytes=MX_ALIGN)
+        nc.vector.tensor_copy(wt_w[:].rearrange("p t m -> p m t"), wt_word_win[:].bitcast(U32).indirect(wt_list[:]))
+        vs_w = keep.tile([P, 2 * N], U8, name="vs_w", align_bytes=MX_ALIGN)
+        nc.vector.tensor_copy(vs_w[:].bitcast(U16), vs_word_win[:].bitcast(U16).indirect(vs_list[:]))
+        vs_s = keep.tile([P, N], U8, name="vs_s", align_bytes=MX_ALIGN)
+        nc.vector.tensor_copy(vs_s[:], vs_scale_win[:].bitcast(U8).indirect(vs_list[:]))
+
+        def half_of(list_tile, h):
+            return list_tile[:, h * HALF_COLS : (h + 1) * HALF_COLS]
+
         xcd = []
-
-        def read_slots(t, h):
-            nc.scalar.activation(xc[h][:, t, :], xcd[t][:].indirect(l2[:, h * hc : (h + 1) * hc]), COPY, scale=gb_t[h][:, t : t + 1])
-
-        for t in range(PACK):
+        for t in range(PLANES):
             tl = keep.tile([P, U], F32, name="xcd%d" % t)
-            nc.scalar.activation(tl[:], ta_t[t][:].indirect(l1[:]), COPY, scale=ga_t[:, t : t + 1])
+            nc.scalar.activation(tl[:], table[t][:].indirect(spell_list[:]), COPY, scale=ga_t[:, t : t + 1])
             xcd.append(tl)
-        xc.append(keep.tile([P, PACK, HALF], BF16, name="xc0", tag="ta2"))
-        for t in range(PACK):
-            read_slots(t, 0)
 
-        place = {(0, 0): (0, 0), (1, 0): (0, 1), (0, 1): (1, 0), (1, 1): (1, 1),
-                 (2, 0): (2, 0), (2, 1): (2, 1), (3, 0): (3, 0), (3, 1): (3, 1)}
-        acc = [psum.tile([P, 2, HALF], F32, name="acc%d" % b) for b in range(4)]
+        xc = [[keep.tile([P, 2, HALF], BF16, name="xc0_%d" % u, tag="ta%d" % (2 + u)) for u in range(2)]]
 
-        def first_product(h):
-            woven = keep.tile([P, HALF, PACK], BF16, name="xw%d" % h, tag="vs_swin", align_bytes=64)
-            for t0, t1 in ((0, 2), (2, 4)):
+        def read_slots(h):
+            for t in range(PLANES):
+                window = xcd[t][:].indirect(half_of(slot_list, h))
+                nc.scalar.activation(xc[h][t // 2][:, t % 2, :], window, COPY, scale=gb_t[h][:, t : t + 1])
+
+        read_slots(0)
+
+        acc = [[psum.tile([P, HALF], F32, name="acc0_%d" % t)[:, :] for t in range(PLANES)]]
+        acc_pairs = [psum.tile([P, 2, HALF], F32, name="acc1_%d" % u) for u in range(2)]
+        acc.append([acc_pairs[t // 2][:, t % 2, :] for t in range(PLANES)])
+
+        def first_product(h, plane_order):
+            woven = keep.tile([P, HALF, PLANES], BF16, name="woven%d" % h, tag="vs_scale_win", align_bytes=MX_ALIGN)
+            for u in range(2):
                 nc.vector.tensor_copy(
-                    woven[:, :, t0:t1].rearrange("p (c i) t -> p c t i", i=4),
-                    xc[h][:, t0:t1, :].rearrange("p t (c i) -> p c t i", i=4),
+                    woven[:, :, 2 * u : 2 * u + 2].rearrange("p (c i) t -> p c t i", i=4),
+                    xc[h][u][:, :, :].rearrange("p t (c i) -> p c t i", i=4),
                 )
-            codes = keep.tile([P, HALF], U32, name="xq%d" % h, align_bytes=64)
-            scales = keep.tile([P, HALF], U8, name="xs%d" % h, align_bytes=64)
+            codes = keep.tile([P, HALF], U32, name="xc_codes%d" % h, align_bytes=MX_ALIGN)
+            scales = keep.tile([P, HALF], U8, name="xc_scales%d" % h, align_bytes=MX_ALIGN)
             nc.vector.quantize_mx(out=codes[:].bitcast(FP8X4), scales=scales[:], in_=woven[:].rearrange("p c t -> p (c t)"))
-            for t in range(PACK):
+            for t in plane_order:
                 nc.tensor.matmul_mx(
-                    out=acc[place[t, h][0]][:, place[t, h][1], :], lhsT=wt_w[:, t, :].bitcast(FP8X4), lhsT_scale=wt_s[:, t, :],
+                    out=acc[h][t], lhsT=wt_w[:, t, :].bitcast(FP8X4), lhsT_scale=wt_s[:, t, :],
                     rhs=codes[:].bitcast(FP8X4), rhs_scale=scales[:], start=True, stop=True,
                 )
 
-        first_product(0)
-        xc.append(keep.tile([P, PACK, HALF], BF16, name="xc1", tag="gb0"))
-        for t in range(PACK):
-            read_slots(t, 1)
-        first_product(1)
+        first_product(0, (0, 1, 3, 2))
+        xc_second = keep.tile([P, PLANES, HALF], BF16, name="xc1", tag="gb0")
+        xc.append([xc_second[:, 0:2, :], xc_second[:, 2:4, :]])
+        read_slots(1)
+        first_product(1, range(PLANES))
 
-        a = [keep.tile([P, 2, HALF], F32, name="a%d" % b) for b in range(4)]
+        a = [[keep.tile([P, HALF], F32, name="a0_%d" % t)[:, :] for t in range(PLANES)]]
+        a_pairs = [keep.tile([P, 2, HALF], F32, name="a1_%d" % u) for u in range(2)]
+        a.append([a_pairs[t // 2][:, t % 2, :] for t in range(PLANES)])
 
-        def put(t, h, on_scalar):
-            dst = pw[t][:].indirect(l4[:, h * hc : (h + 1) * hc])
-            src = a[place[t, h][0]][:, place[t, h][1], :]
-            if on_scalar:
-                nc.scalar.activation(dst, src, COPY)
-            else:
-                nc.vector.tensor_copy(dst, src)
+        def put_on_scalar(t, h):
+            nc.scalar.activation(board[t][:].indirect(half_of(put_list, h)), a[h][t], COPY)
 
-        first = keep.tile([P, PACK, O], F32, name="first")
-        second = keep.tile([P, PACK, O], F32, name="second")
-        diff = keep.tile([P, PACK, O], F32, name="diff")
+        def put_on_vector(t, h):
+            nc.vector.tensor_copy(board[t][:].indirect(half_of(put_list, h)), a[h][t])
+
+        first = keep.tile([P, PLANES, O], F32, name="first")
+        second = keep.tile([P, PLANES, O], F32, name="second")
+        diff = keep.tile([P, PLANES, O], F32, name="diff")
+        hid = keep.tile([P, O, PLANES], BF16, name="hid", align_bytes=MX_ALIGN)
 
         def read_board(t):
-            nc.scalar.activation(first[:, t, :], pw[t][:].indirect(l5[:]), COPY, scale=sa_t[:, t : t + 1])
-            nc.scalar.activation(second[:, t, :], pw[t][:].indirect(l6[:]), COPY, scale=sb_t[:, t : t + 1])
+            nc.scalar.activation(first[:, t, :], board[t][:].indirect(first_list[:]), COPY, scale=sa_t[:, t : t + 1])
+            nc.scalar.activation(second[:, t, :], board[t][:].indirect(second_list[:]), COPY, scale=sb_t[:, t : t + 1])
 
-        hid = keep.tile([P, O, PACK], BF16, name="hid", align_bytes=64)
-        for u in range(2):
-            nc.scalar.copy(a[0][:, u, :], acc[0][:, u, :])
-        put(0, 0, True)
-        put(1, 0, False)
-        for u in range(2):
-            nc.scalar.copy(a[1][:, u, :], acc[1][:, u, :])
-        nc.vector.tensor_copy(a[2][:], acc[2][:])
-        nc.vector.tensor_copy(a[3][:], acc[3][:])
-        put(0, 1, True)
-        put(1, 1, False)
-        put(3, 0, True)
-        nc.vector.tensor_copy(pw[2][:].indirect(l4[:]), a[2][:].rearrange("p h j -> p (h j)"))
+        def subtract(planes):
+            nc.vector.tensor_tensor(diff[:, planes, :], first[:, planes, :], second[:, planes, :], SUB)
+
+        for t in (0, 1, 3):
+            nc.scalar.copy(a[0][t], acc[0][t])
+        nc.vector.tensor_copy(a[0][2], acc[0][2])
+        put_on_scalar(0, 0)
+        put_on_vector(1, 0)
+        put_on_scalar(3, 0)
+        put_on_vector(2, 0)
+        for t in (0, 1):
+            nc.scalar.copy(a[1][t], acc[1][t])
+        nc.vector.tensor_copy(a_pairs[1][:], acc_pairs[1][:])
+        put_on_scalar(0, 1)
+        put_on_vector(1, 1)
         read_board(0)
-        put(3, 1, False)
+        put_on_vector(2, 1)
+        put_on_vector(3, 1)
         read_board(1)
-        nc.vector.tensor_tensor(diff[:, 0:2, :], first[:, 0:2, :], second[:, 0:2, :], SUB)
+        subtract(slice(0, 2))
         read_board(2)
-        nc.vector.tensor_tensor(diff[:, 2, :], first[:, 2, :], second[:, 2, :], SUB)
-        low = diff[:, 0:2, :].rearrange("p t o -> p o t")
-        nc.vector.scalar_tensor_tensor(hid[:, :, 0:2], low, -1.0, low, MULT, MAX)
+        subtract(2)
+        low_pair = diff[:, 0:2, :].rearrange("p t o -> p o t")
+        nc.vector.scalar_tensor_tensor(hid[:, :, 0:2], low_pair, -1.0, low_pair, MULT, MAX)
         read_board(3)
-        nc.vector.tensor_tensor(diff[:, 3, :], first[:, 3, :], second[:, 3, :], SUB)
+        subtract(3)
         nc.scalar.activation(hid[:, :, 2:4], diff[:, 2:4, :].rearrange("p t o -> p o t"), ABS)
-        hq = keep.tile([P, O], U32, name="hq", align_bytes=64)
-        hs = keep.tile([P, O], U8, name="hs", align_bytes=64)
-        nc.vector.quantize_mx(out=hq[:].bitcast(FP8X4), scales=hs[:], in_=hid[:].rearrange("p c t -> p (c t)"))
-        for i in range(2):
+
+        hid_codes = keep.tile([P, O], U32, name="hid_codes", align_bytes=MX_ALIGN)
+        hid_scales = keep.tile([P, O], U8, name="hid_scales", align_bytes=MX_ALIGN)
+        nc.vector.quantize_mx(out=hid_codes[:].bitcast(FP8X4), scales=hid_scales[:], in_=hid[:].rearrange("p c t -> p (c t)"))
+
+        for i, (copy_out, queue) in enumerate(((nc.vector.tensor_copy, nc.sync), (nc.scalar.copy, nc.scalar))):
+            rows = slice(P * i, P * (i + 1))
             y = psum.tile([P, O], F32, name="y%d" % i)
             nc.tensor.matmul_mx(
-                out=y[:], lhsT=vs_w[:, 2 * P * i : 2 * P * (i + 1)].bitcast(FP4X4), lhsT_scale=vs_s[:, P * i : P * (i + 1)],
-                rhs=hq[:].bitcast(FP8X4), rhs_scale=hs[:], start=True, stop=True,
+                out=y[:], lhsT=vs_w[:, 2 * P * i : 2 * P * (i + 1)].bitcast(FP4X4), lhsT_scale=vs_s[:, rows],
+                rhs=hid_codes[:].bitcast(FP8X4), rhs_scale=hid_scales[:], start=True, stop=True,
             )
             res = keep.tile([P, O], F32, name="res%d" % i)
-            if i == 0:
-                nc.vector.tensor_copy(res[:], y[:])
-                nc.sync.dma_start(out[P * i : P * (i + 1), :], res[:])
-            else:
-                nc.scalar.copy(res[:], y[:])
-                nc.scalar.dma_start(out[P * i : P * (i + 1), :], res[:])
+            copy_out(res[:], y[:])
+            queue.dma_start(out[rows, :], res[:])

from contextlib import ExitStack

import concourse.mybir as mybir

K, J, R, T, U, F, C, O, N, S = 512, 256, 512, 1024, 512, 1024, 512, 128, 256, 1024
FLOPS = 2 * K * R * J + 2 * R * N * O

F32 = mybir.dt.float32
BF16 = mybir.dt.bfloat16
I32 = mybir.dt.int32
U32 = mybir.dt.uint32
U16 = mybir.dt.uint16
U8 = mybir.dt.uint8
FP8X4 = mybir.dt.float8_e4m3fn_x4
FP4X4 = mybir.dt.float4_e2m1fn_x4
COPY = mybir.ActivationFunctionType.Copy
ABS = mybir.ActivationFunctionType.Abs
SUB = mybir.AluOpType.subtract
MULT = mybir.AluOpType.mult
MAX = mybir.AluOpType.max

P = 128
PLANES = 4
QUADRANT = 32
HALF = J // 2
HALF_COLS = HALF // 16
MX_ALIGN = 64


def tile_picked_respelled_store_one_boardmixed_store_plain_kernel(
    tc, ta, ga, gb, wt_words, wt_scales, sa, sb, vs_words, vs_scales, offs, offs2, offs3, offs4, offs5, offs6, offs7, out
):
    nc = tc.nc
    with ExitStack() as ctx:
        lists = ctx.enter_context(tc.tile_pool(name="lists", bufs=1))
        keep = ctx.enter_context(tc.tile_pool(name="keep", bufs=1))
        psum = ctx.enter_context(tc.psum_pool(name="psum", bufs=1))

        def load_list(src, name):
            tl = lists.tile([P, src.shape[1]], U16, name=name)
            nc.sync.dma_start(tl[:], src)
            return tl

        def load_row_values(src, name, queue):
            tl = keep.tile([P, PLANES], F32, name=name, tag=name)
            queue.dma_start(tl[:], src.rearrange("(p t) o -> p (t o)", t=PLANES))
            return tl

        ta_rows = ta.rearrange("(p t) c -> p t c", t=PLANES)

        def load_table_plane(t):
            tl = keep.tile([P, T], F32, name="ta%d" % t, tag="ta%d" % t)
            nc.sync.dma_start(tl[:], ta_rows[:, t, :])
            return tl

        def load_scale_rows(src, name, clearing_engine):
            tl = keep.tile([P, src.shape[2] // 4], I32, name=name, tag=name, align_bytes=MX_ALIGN)
            clearing_engine.memset(tl[:], 0)
            rows = src[0].rearrange("(q j) c -> j q c", j=4).bitcast(I32)
            for j in range(4):
                nc.sync.dma_start(tl[j:P:QUADRANT, :], rows[j])
            return tl

        warm = keep.tile([P, 2], F32, name="warm")
        nc.gpsimd.memset(warm[:, 0:1], 0.0)
        nc.scalar.activation(warm[:, 1:2], warm[:, 0:1], COPY)

        spell_list = load_list(offs, "spell_list")
        ga_t = load_row_values(ga, "ga_t", nc.scalar)
        table = [load_table_plane(0), load_table_plane(1)]
        wt_scale_win = load_scale_rows(wt_scales, "wt_scale_win", nc.gpsimd)
        wt_list = load_list(offs3, "wt_list")
        table.append(load_table_plane(2))
        wt_word_win = keep.tile([P, F], I32, name="wt_word_win")
        nc.sync.dma_start(wt_word_win[:], wt_words[0].rearrange("p n t -> p (n t)").bitcast(I32))
        slot_list = load_list(offs2, "slot_list")
        gb_t = [load_row_values(gb, "gb0", nc.sync)]
        table.append(load_table_plane(3))
        vs_list = load_list(offs7, "vs_list")
        vs_word_win = keep.tile([P, S // 2], I32, name="vs_word_win")
        nc.sync.dma_start(vs_word_win[:], vs_words[0].bitcast(I32))
        vs_scale_win = load_scale_rows(vs_scales, "vs_scale_win", nc.vector)
        put_list = load_list(offs4, "put_list")
        first_list = load_list(offs5, "first_list")
        second_list = load_list(offs6, "second_list")
        sa_t = load_row_values(sa, "sa_t", nc.sync)
        sb_t = load_row_values(sb, "sb_t", nc.sync)
        gb_t.append(keep.tile([P, PLANES], F32, name="gb1"))
        nc.vector.tensor_copy(gb_t[1][:], gb_t[0][:])

        board = []
        for t in range(PLANES):
            tl = keep.tile([P, C], F32, name="board%d" % t)
            nc.vector.memset(tl[:], 0.0)
            board.append(tl)

        wt_s = keep.tile([P, PLANES, P], U8, name="wt_s", align_bytes=MX_ALIGN)
        nc.vector.tensor_copy(wt_s[:].rearrange("p t m -> p m t"), wt_scale_win[:].bitcast(U8).indirect(wt_list[:]))
        wt_w = keep.tile([P, PLANES, P], U32, name="wt_w", align_bytes=MX_ALIGN)
        nc.vector.tensor_copy(wt_w[:].rearrange("p t m -> p m t"), wt_word_win[:].bitcast(U32).indirect(wt_list[:]))
        vs_w = keep.tile([P, 2 * N], U8, name="vs_w", align_bytes=MX_ALIGN)
        nc.vector.tensor_copy(vs_w[:].bitcast(U16), vs_word_win[:].bitcast(U16).indirect(vs_list[:]))
        vs_s = keep.tile([P, N], U8, name="vs_s", align_bytes=MX_ALIGN)
        nc.vector.tensor_copy(vs_s[:], vs_scale_win[:].bitcast(U8).indirect(vs_list[:]))

        def half_of(list_tile, h):
            return list_tile[:, h * HALF_COLS : (h + 1) * HALF_COLS]

        xcd = []
        for t in range(PLANES):
            tl = keep.tile([P, U], F32, name="xcd%d" % t)
            nc.scalar.activation(tl[:], table[t][:].indirect(spell_list[:]), COPY, scale=ga_t[:, t : t + 1])
            xcd.append(tl)

        xc = [[keep.tile([P, 2, HALF], BF16, name="xc0_%d" % u, tag="ta%d" % (2 + u)) for u in range(2)]]

        def read_slots(h):
            for t in range(PLANES):
                window = xcd[t][:].indirect(half_of(slot_list, h))
                nc.scalar.activation(xc[h][t // 2][:, t % 2, :], window, COPY, scale=gb_t[h][:, t : t + 1])

        read_slots(0)

        acc = [[psum.tile([P, HALF], F32, name="acc0_%d" % t)[:, :] for t in range(PLANES)]]
        acc_pairs = [psum.tile([P, 2, HALF], F32, name="acc1_%d" % u) for u in range(2)]
        acc.append([acc_pairs[t // 2][:, t % 2, :] for t in range(PLANES)])

        def first_product(h, plane_order):
            woven = keep.tile([P, HALF, PLANES], BF16, name="woven%d" % h, tag="vs_scale_win", align_bytes=MX_ALIGN)
            for u in range(2):
                nc.vector.tensor_copy(
                    woven[:, :, 2 * u : 2 * u + 2].rearrange("p (c i) t -> p c t i", i=4),
                    xc[h][u][:, :, :].rearrange("p t (c i) -> p c t i", i=4),
                )
            codes = keep.tile([P, HALF], U32, name="xc_codes%d" % h, align_bytes=MX_ALIGN)
            scales = keep.tile([P, HALF], U8, name="xc_scales%d" % h, align_bytes=MX_ALIGN)
            nc.vector.quantize_mx(out=codes[:].bitcast(FP8X4), scales=scales[:], in_=woven[:].rearrange("p c t -> p (c t)"))
            for t in plane_order:
                nc.tensor.matmul_mx(
                    out=acc[h][t], lhsT=wt_w[:, t, :].bitcast(FP8X4), lhsT_scale=wt_s[:, t, :],
                    rhs=codes[:].bitcast(FP8X4), rhs_scale=scales[:], start=True, stop=True,
                )

        first_product(0, (0, 1, 3, 2))
        xc_second = keep.tile([P, PLANES, HALF], BF16, name="xc1", tag="gb0")
        xc.append([xc_second[:, 0:2, :], xc_second[:, 2:4, :]])
        read_slots(1)
        first_product(1, range(PLANES))

        a = [[keep.tile([P, HALF], F32, name="a0_%d" % t)[:, :] for t in range(PLANES)]]
        a_pairs = [keep.tile([P, 2, HALF], F32, name="a1_%d" % u) for u in range(2)]
        a.append([a_pairs[t // 2][:, t % 2, :] for t in range(PLANES)])

        def put_on_scalar(t, h):
            nc.scalar.activation(board[t][:].indirect(half_of(put_list, h)), a[h][t], COPY)

        def put_on_vector(t, h):
            nc.vector.tensor_copy(board[t][:].indirect(half_of(put_list, h)), a[h][t])

        first = keep.tile([P, PLANES, O], F32, name="first")
        second = keep.tile([P, PLANES, O], F32, name="second")
        diff = keep.tile([P, PLANES, O], F32, name="diff")
        hid = keep.tile([P, O, PLANES], BF16, name="hid", align_bytes=MX_ALIGN)

        def read_board(t):
            nc.scalar.activation(first[:, t, :], board[t][:].indirect(first_list[:]), COPY, scale=sa_t[:, t : t + 1])
            nc.scalar.activation(second[:, t, :], board[t][:].indirect(second_list[:]), COPY, scale=sb_t[:, t : t + 1])

        def subtract(planes):
            nc.vector.tensor_tensor(diff[:, planes, :], first[:, planes, :], second[:, planes, :], SUB)

        for t in (0, 1, 3):
            nc.scalar.copy(a[0][t], acc[0][t])
        nc.vector.tensor_copy(a[0][2], acc[0][2])
        put_on_scalar(0, 0)
        put_on_vector(1, 0)
        put_on_scalar(3, 0)
        put_on_vector(2, 0)
        for t in (0, 1):
            nc.scalar.copy(a[1][t], acc[1][t])
        nc.vector.tensor_copy(a_pairs[1][:], acc_pairs[1][:])
        put_on_scalar(0, 1)
        put_on_vector(1, 1)
        read_board(0)
        put_on_vector(2, 1)
        put_on_vector(3, 1)
        read_board(1)
        subtract(slice(0, 2))
        read_board(2)
        subtract(2)
        low_pair = diff[:, 0:2, :].rearrange("p t o -> p o t")
        nc.vector.scalar_tensor_tensor(hid[:, :, 0:2], low_pair, -1.0, low_pair, MULT, MAX)
        read_board(3)
        subtract(3)
        nc.scalar.activation(hid[:, :, 2:4], diff[:, 2:4, :].rearrange("p t o -> p o t"), ABS)

        hid_codes = keep.tile([P, O], U32, name="hid_codes", align_bytes=MX_ALIGN)
        hid_scales = keep.tile([P, O], U8, name="hid_scales", align_bytes=MX_ALIGN)
        nc.vector.quantize_mx(out=hid_codes[:].bitcast(FP8X4), scales=hid_scales[:], in_=hid[:].rearrange("p c t -> p (c t)"))

        for i, (copy_out, queue) in enumerate(((nc.vector.tensor_copy, nc.sync), (nc.scalar.copy, nc.scalar))):
            rows = slice(P * i, P * (i + 1))
            y = psum.tile([P, O], F32, name="y%d" % i)
            nc.tensor.matmul_mx(
                out=y[:], lhsT=vs_w[:, 2 * P * i : 2 * P * (i + 1)].bitcast(FP4X4), lhsT_scale=vs_s[:, rows],
                rhs=hid_codes[:].bitcast(FP8X4), rhs_scale=hid_scales[:], start=True, stop=True,
            )
            res = keep.tile([P, O], F32, name="res%d" % i)
            copy_out(res[:], y[:])
            queue.dma_start(out[rows, :], res[:])
